import numpy as np
import ml_dtypes


def mxq(x, axis, fmt="e4m3"):
    dtype, down = {"e4m3": (ml_dtypes.float8_e4m3fn, 7), "e5m2": (ml_dtypes.float8_e5m2, 14)}[fmt]
    v = np.moveaxis(np.asarray(x, np.float32).astype(ml_dtypes.bfloat16).astype(np.float64), axis, -1)
    blocks = v.reshape(v.shape[:-1] + (-1, 32))
    amax = np.abs(blocks).max(-1, keepdims=True)
    byte = np.maximum(np.where(amax > 0, np.frexp(amax)[1] - 1 + 127, 0) - down, 1)
    scale = np.exp2(byte - 127.0)
    codes = (blocks / scale).astype(np.float32).astype(dtype).astype(np.float64)
    return np.moveaxis((codes * scale).reshape(v.shape), -1, axis)


WIDE = False


def mx_kscale(k):
    if not WIDE:
        return np.ones(k)
    levels = np.array([10, -10, 5, -5, 0])
    if k % 512:
        return np.exp2(np.random.permutation(np.resize(levels, k // 32))).repeat(32)
    a = np.empty((k // 512, 16))
    for p in range(k // 512):
        a[p, :8] = np.random.permutation(np.resize(levels, 8))
        for g in range(8):
            far = levels[np.abs(levels - a[p, g]) >= 10]
            a[p, g + 8] = far[np.random.randint(len(far))]
    return np.exp2(a.ravel()).repeat(32)


BF16 = ml_dtypes.bfloat16


def bf(x):
    return np.asarray(x, np.float32).astype(BF16)


def f64(x):
    return np.asarray(x).astype(np.float64)


E2M1 = np.array([0.0, 0.5, 1.0, 1.5, 2.0, 3.0, 4.0, 6.0, -0.0, -0.5, -1.0, -1.5, -2.0, -3.0, -4.0, -6.0])


def pack_weight(w, fmt):
    k, n = w.shape
    w = f64(bf(w)).reshape(k // 32, 32, n)
    amax = np.abs(w).max(1)
    if fmt == "e4m3":
        byte = np.frexp(amax)[1] - 1 + 127 - 7
    else:
        mant, ex = np.frexp(amax / 6.0)
        byte = np.where(mant > 0.5, ex, ex - 1) + 127
    byte = np.clip(np.where(amax > 0, byte, 1), 1, 254)
    scaled = (w * np.exp2(127.0 - byte)[:, None, :]).reshape(k, n).astype(np.float32)
    by_word = np.ascontiguousarray(scaled.reshape(k // 512, 128, 4, n).transpose(0, 1, 3, 2))
    if fmt == "e4m3":
        words = by_word.astype(ml_dtypes.float8_e4m3fn).view(np.uint8)
    else:
        c = by_word.astype(ml_dtypes.float4_e2m1fn).view(np.uint8) & 0xF
        words = c[..., 0::2] | (c[..., 1::2] << 4)
    return np.ascontiguousarray(words), np.ascontiguousarray(byte.astype(np.uint8).reshape(k // 512, 16, n))


def unpack_weight(words, scales, fmt):
    g, p, n, _ = words.shape
    if fmt == "e4m3":
        vals = np.ascontiguousarray(words).view(ml_dtypes.float8_e4m3fn).astype(np.float64)
    else:
        nib = np.empty((g, p, n, 4), np.uint8)
        nib[..., 0::2] = words & 0xF
        nib[..., 1::2] = words >> 4
        vals = E2M1[nib]
    vals = vals * np.repeat(np.exp2(scales.astype(np.float64) - 127.0), 8, axis=1)[..., None]
    return vals.transpose(0, 1, 3, 2).reshape(g * 512, n)
def pack4(w):
    words, scales = pack_weight(w, "e2m1")
    return words.reshape(words.shape[0], 128, -1), scales


def unpack4(words, scales):
    return unpack_weight(words.reshape(words.shape[0], 128, -1, 2), scales, "e2m1")


G, M, K, J, R, L = 4, 1024, 512, 1024, 512, 4


def setup_inputs():
    s = mx_kscale(G * K).reshape(G, K)
    t = mx_kscale(G * J).reshape(G, J)
    z = np.random.standard_normal((G, M + J, L))
    f = np.tile(z, (1, 1, K // L)) * np.sign(np.random.standard_normal((G, 1, K)))
    f = f + 0.6 * np.random.standard_normal((G, M + J, K))
    f = f / np.sqrt(np.square(f).sum(-1, keepdims=True))
    r = 0.5 + 0.5 * np.sqrt(np.square(z[:, M:]).mean(-1))
    c = f[:, M:] * r[:, :, None]
    y = 2 * z + np.random.standard_normal((G, M + J, L))
    b = np.sqrt(np.square(y[:, M:, None, :] - y[:, None, :R, :]).sum(-1))
    b = b - b.mean(1, keepdims=True) - b.mean(2, keepdims=True) + b.mean((1, 2), keepdims=True)
    c_words, c_scales = pack4((2 * c.transpose(0, 2, 1) / s[:, :, None] * np.square(t)[:, None, :]).reshape(G * K, J))
    b_words, b_scales = pack4((b / J / t[:, :, None]).reshape(G * J, R))
    m = 0.98 * np.sqrt(1 + np.square(r)) + 0.05 * np.random.standard_normal((G, J))
    return {"x": bf(f[:, :M] * s[:, None, :]),
            "c_words": c_words, "c_scales": c_scales,
            "e": bf((1 + np.square(r)) * np.square(t)),
            "m": bf(m * t),
            "b_words": b_words, "b_scales": b_scales}


def reference(x, c_words, c_scales, e, m, b_words, b_scales):
    c = unpack4(c_words, c_scales).reshape(G, K, J)
    b = unpack4(b_words, b_scales).reshape(G, J, R)
    out = []
    for g in range(G):
        gram = mxq(f64(x)[g], 1, "e4m3") @ c[g]
        d = np.sqrt(f64(e)[g] - gram)
        a = d - f64(m)[g]
        out.append(mxq(a, 1, "e4m3") @ b[g])
    return np.stack(out)

@@ -1,0 +1,337 @@
+from contextlib import ExitStack
+
+import concourse.mybir as mybir
+from concourse.masks import make_identity
+
+F32 = mybir.dt.float32
+BF16 = mybir.dt.bfloat16
+I32 = mybir.dt.int32
+U32 = mybir.dt.uint32
+U8 = mybir.dt.uint8
+FP8X4 = mybir.dt.float8_e4m3fn_x4
+FP4X4 = mybir.dt.float4_e2m1fn_x4
+SQRT = mybir.ActivationFunctionType.Sqrt
+SUB = mybir.AluOpType.subtract
+
+V, M, K, J, R = 4, 1024, 512, 1024, 512
+P = 128
+H = 2
+N = 512
+UNITS = V * H * H
+
+FLOPS = 2 * V * M * J * (K + R)
+
+
+def tile_landmark_distance_cross_covariance_s14_kernel(
+    tc, x, c_words, c_scales, e, m, b_words, b_scales, out
+):
+    nc = tc.nc
+    with ExitStack() as ctx:
+        keep = ctx.enter_context(tc.tile_pool(name="keep", bufs=1))
+        work = ctx.enter_context(tc.tile_pool(name="work", bufs=2))
+        psum = ctx.enter_context(tc.psum_pool(name="psum", bufs=1))
+        ctx.enter_context(tc.manual_schedule())
+
+        ident = keep.tile([P, P], F32, name="ident")
+        warm = keep.tile([P, 1], F32, name="warm")
+        e_sb = keep.tile([P, V * H, 4], BF16, name="e_sb")
+        m_sb = keep.tile([P, V * H, 4], BF16, name="m_sb")
+        c_sc_raw = keep.tile([P, V, J], U8, name="c_sc_raw", align_bytes=64)
+        c_sc = keep.tile([P, V * H, 512], U8, name="c_sc", align_bytes=64)
+        b_sc = keep.tile([P, V * H, R], U8, name="b_sc", align_bytes=64)
+        c_raw = [keep.tile([P, 2 * J], U8, name=f"c_raw{v}", align_bytes=64) for v in range(V)]
+        c_cd = [keep.tile([P, 1024], U8, name=f"c_cd{g}", align_bytes=64) for g in range(V * H)]
+        b_sb = [keep.tile([P, H, 2 * R], U8, name=f"b_sb{v}", align_bytes=64) for v in range(V)]
+        x_sb = [[keep.tile([P, 2, K], BF16, name=f"x{j}_{b}", align_bytes=64) for b in range(2)] for j in range(V * H)]
+
+        def load_x(j, b):
+            v, s = j // 2, j % 2
+            src = x[v, s * N : (s + 1) * N, :].rearrange("(p r) k -> p r k", r=4)
+            nc.sync.dma_start(out=x_sb[j][b][:], in_=src[:, 2 * b : 2 * b + 2, :])
+
+        def load_c(v):
+            nc.sync.dma_start(out=c_raw[v][:].bitcast(I32), in_=c_words[v].bitcast(I32))
+
+        def load_b(v):
+            nc.sync.dma_start(
+                out=b_sb[v][:].bitcast(I32), in_=b_words[2 * v : 2 * v + 2].rearrange("g p n -> p g n").bitcast(I32)
+            )
+
+        def load_scales(plane, src):
+            for q in range(4):
+                nc.sync.dma_start(
+                    out=plane[32 * q : 32 * q + 4].bitcast(I32),
+                    in_=src[:, 4 * q : 4 * q + 4, :].rearrange("g r n -> r g n").bitcast(I32),
+                )
+
+        nc.vector.memset(c_sc_raw[:].rearrange("p v n -> p (v n)").bitcast(I32), 0)
+        nc.gpsimd.memset(warm[:], 1.0)
+        make_identity(nc, ident[:])
+        nc.gpsimd.memset(b_sc[:].rearrange("p g n -> p (g n)").bitcast(I32), 0)
+        e_rows = e.rearrange("v j -> (v j)").rearrange("(g p t) -> p g t", p=P, t=4)
+        m_rows = m.rearrange("v j -> (v j)").rearrange("(g p t) -> p g t", p=P, t=4)
+        nc.scalar.dma_start(out=e_sb[:, :2, :], in_=e_rows[:, :2, :])
+        nc.scalar.activation(out=warm[:], in_=warm[:], func=SQRT)
+
+        load_c(0)
+        load_x(0, 0)
+        load_scales(c_sc_raw, c_scales)
+        load_x(0, 1)
+        nc.sync.dma_start(out=m_sb[:, :2, :], in_=m_rows[:, :2, :])
+        load_x(1, 0)
+        load_x(1, 1)
+        load_c(1)
+        load_x(2, 0)
+        load_x(2, 1)
+        load_b(0)
+        load_scales(b_sc, b_scales)
+        load_x(3, 0)
+        load_x(3, 1)
+        nc.sync.dma_start(out=e_sb[:, 2:, :], in_=e_rows[:, 2:, :])
+        nc.sync.dma_start(out=m_sb[:, 2:, :], in_=m_rows[:, 2:, :])
+        load_c(2)
+        load_c(3)
+        for j in range(4, V * H):
+            load_x(j, 0)
+            load_x(j, 1)
+            if j % 2 == 0:
+                load_b(j // 2 - 1)
+        load_b(3)
+
+        def permute_c(g):
+            v, h = g // 2, g % 2
+            nc.vector.tensor_copy(
+                out=c_cd[g][:].rearrange("p (t m b) -> p t m b", t=4, b=2),
+                in_=c_raw[v][:, h * 1024 : (h + 1) * 1024].rearrange("p (m t b) -> p t m b", t=4, b=2),
+            )
+
+        def permute_c_scales(g):
+            v, h = g // 2, g % 2
+            nc.vector.tensor_copy(
+                out=c_sc[:, g, :].rearrange("p (t m) -> p t m", t=4),
+                in_=c_sc_raw[:, v, h * 512 : (h + 1) * 512].rearrange("p (m t) -> p t m", t=4),
+            )
+
+        banks = {}
+
+        def transpose_x(j, b):
+            xp = psum.tile([P, 2, 2, P], F32, name="xp", bufs=2)
+            words = x_sb[j][b][:].rearrange("p r k -> p (r k)").bitcast(F32)
+            for rr in range(2):
+                for u in range(2):
+                    nc.tensor.transpose(xp[:, rr, u, :], words[:, 256 * rr + u : 256 * (rr + 1) : 2], ident[:])
+            banks[j, b] = xp
+
+        grouped = {}
+        xq = {}
+
+        def empty_x(j, b, eng):
+            if j not in grouped:
+                grouped[j] = work.tile([P, N, 4], BF16, name="grouped", align_bytes=64)
+            dst = grouped[j][:].rearrange("p n t -> p (n t)").bitcast(F32)[:, b * 512 : (b + 1) * 512]
+            dst = dst.rearrange("p (r s u) -> p r s u", r=2, u=2)
+            src = banks[j, b][:].rearrange("p r u s -> p r s u")
+            if eng == "v":
+                nc.vector.tensor_copy(out=dst, in_=src)
+            else:
+                nc.scalar.copy(out=dst, in_=src)
+
+        def quantize_x(j, n0=0, n1=N):
+            if n0 == 0:
+                codes = work.tile([P, N], U32, name="xq", align_bytes=64)
+                scales = work.tile([P, N], U8, name="xqs", align_bytes=64)
+                xq[j] = (codes, scales)
+            codes, scales = xq[j]
+            nc.vector.quantize_mx(
+                out=codes[:, n0:n1].bitcast(FP8X4),
+                scales=scales[:, n0:n1],
+                in_=grouped[j][:, n0:n1, :].rearrange("p n t -> p (n t)"),
+            )
+
+        gram = {}
+        dist = {}
+        cent = {}
+        aq = {}
+
+        def stage1(k):
+            j, h, n0, n1 = pieces[k]
+            g = (j // 2) * 2 + h
+            codes, scales = xq[j]
+            for t in range(4):
+                acc = psum.tile([P, N], F32, name="gram", bufs=4)
+                nc.tensor.matmul_mx(
+                    out=acc[:, : n1 - n0],
+                    lhsT=c_cd[g][:, 256 * t : 256 * (t + 1)].bitcast(FP4X4),
+                    lhsT_scale=c_sc[:, g, 128 * t : 128 * (t + 1)],
+                    rhs=codes[:, n0:n1].bitcast(FP8X4),
+                    rhs_scale=scales[:, n0:n1],
+                    start=True,
+                    stop=True,
+                )
+                gram[k, t] = acc
+
+        def root(k):
+            j, h, n0, n1 = pieces[k]
+            g = (j // 2) * 2 + h
+            dist[k] = work.tile([P, 4, N], F32, name="dist", bufs=3)
+            for t in range(4):
+                nc.scalar.activation(
+                    out=dist[k][:, t, : n1 - n0],
+                    in_=gram[k, t][:, : n1 - n0],
+                    func=SQRT,
+                    bias=e_sb[:, g, t : t + 1],
+                    scale=-1.0,
+                )
+
+        def centre(k, a, b):
+            j, h, n0, n1 = pieces[k]
+            g = (j // 2) * 2 + h
+            if a == 0:
+                cent[k] = work.tile([P, N, 4], BF16, name="cent", align_bytes=64)
+            nc.vector.tensor_tensor(
+                out=cent[k][:, a:b, :].rearrange("p (c i) t -> p c t i", i=4),
+                in0=dist[k][:, :, a:b].rearrange("p t (c i) -> p c t i", i=4),
+                in1=m_sb[:, g, :].unsqueeze(1).unsqueeze(3).to_broadcast([P, (b - a) // 4, 4, 4]),
+                op=SUB,
+            )
+
+        def quantize_a(k, a, b):
+            j, h, n0, n1 = pieces[k]
+            if (j, h) not in aq:
+                codes = work.tile([P, N], U32, name="aq", align_bytes=64, bufs=6)
+                scales = work.tile([P, N], U8, name="aqs", align_bytes=64, bufs=6)
+                aq[j, h] = (codes, scales)
+            codes, scales = aq[j, h]
+            nc.vector.quantize_mx(
+                out=codes[:, n0 + a : n0 + b].bitcast(FP8X4),
+                scales=scales[:, n0 + a : n0 + b],
+                in_=cent[k][:, a:b, :].rearrange("p n t -> p (n t)"),
+            )
+
+        cov = {}
+        rows = {}
+
+        def stage2(j, r, name="cov", bufs=2):
+            acc = psum.tile([P, R], F32, name=name, bufs=bufs)
+            v = j // 2
+            for h in range(H):
+                codes, scales = aq[j, h]
+                nc.tensor.matmul_mx(
+                    out=acc[:],
+                    lhsT=codes[:, P * r : P * (r + 1)].bitcast(FP8X4),
+                    lhsT_scale=scales[:, P * r : P * (r + 1)],
+                    rhs=b_sb[v][:, h, :].bitcast(FP4X4),
+                    rhs_scale=b_sc[:, 2 * v + h, :],
+                    start=(h == 0),
+                    stop=(h == H - 1),
+                )
+            cov[j, r] = acc
+
+        def empty_out(j, r, eng):
+            if (j, r // 2) not in rows:
+                rows[j, r // 2] = work.tile([P, 2, R], F32, name="rows", bufs=4)
+            dst = rows[j, r // 2][:, r % 2, :]
+            if eng == "v":
+                nc.vector.tensor_copy(out=dst, in_=cov[j, r][:])
+            else:
+                nc.scalar.copy(out=dst, in_=cov[j, r][:])
+
+        def store(j, b):
+            v, s = j // 2, j % 2
+            dst = out[v, s * N : (s + 1) * N, :].rearrange("(p r) c -> p r c", r=4)
+            nc.sync.dma_start(out=dst[:, 2 * b : 2 * b + 2, :], in_=rows[j, b][:])
+
+        LAST = V * H - 1
+        pieces = []
+        for j in range(V * H):
+            if j == 0:
+                pieces += [(0, 0, 0, 256), (0, 0, 256, N), (0, 1, 0, N)]
+            elif j == LAST:
+                pieces += [(j, 0, 0, 256), (j, 1, 0, 256), (j, 0, 256, N), (j, 1, 256, N)]
+            else:
+                pieces += [(j, 0, 0, N), (j, 1, 0, N)]
+
+        transpose_x(0, 0)
+        transpose_x(0, 1)
+        permute_c(0)
+        permute_c_scales(0)
+        empty_x(0, 0, "s")
+        empty_x(0, 1, "s")
+        quantize_x(0, 0, 256)
+        quantize_x(0, 256, N)
+        stage1(0)
+        permute_c(1)
+        permute_c_scales(1)
+        transpose_x(1, 0)
+        transpose_x(1, 1)
+
+        filler = {}
+        for g in range(2, V * H):
+            filler[g - 2 if g < 4 else 2 * g - 4] = g
+
+        done = []
+        for k, (j, h, n0, n1) in enumerate(pieces):
+            pos = len([p for p in pieces[:k] if p[0] == j])
+            first = pos == 0
+            second = pos == (2 if j == 0 else 1)
+            todo = None
+            if second and j >= 1:
+                todo = (j - 1, 0)
+            elif first and j >= 2:
+                todo = (j - 2, 1)
+            elif j == LAST and pos == 2:
+                todo = (j - 1, 1)
+            if todo:
+                stage2(todo[0], 2 * todo[1])
+                stage2(todo[0], 2 * todo[1] + 1)
+            if first and j + 2 <= LAST:
+                transpose_x(j + 2, 0)
+                transpose_x(j + 2, 1)
+            root(k)
+            if k == 0:
+                empty_x(1, 0, "s")
+                empty_x(1, 1, "s")
+            if todo:
+                empty_out(todo[0], 2 * todo[1], "s")
+                empty_out(todo[0], 2 * todo[1] + 1, "s")
+                store(*todo)
+            split = not ((first and j + 1 <= LAST) or (second and j + 2 <= LAST))
+            if k >= 1:
+                w = pieces[k - 1][3] - pieces[k - 1][2]
+                if split:
+                    centre(k - 1, 0, w // 2)
+                    centre(k - 1, w // 2, w)
+                else:
+                    centre(k - 1, 0, w)
+            if first and j + 1 <= LAST:
+                quantize_x(j + 1)
+            if second and j + 2 <= LAST:
+                empty_x(j + 2, 0, "v")
+                empty_x(j + 2, 1, "s")
+            if k in filler:
+                permute_c(filler[k])
+                permute_c_scales(filler[k])
+            if k >= 1:
+                if split:
+                    quantize_a(k - 1, 0, w // 2)
+                    quantize_a(k - 1, w // 2, w)
+                else:
+                    quantize_a(k - 1, 0, w)
+            if k + 1 < len(pieces):
+                stage1(k + 1)
+
+        k = len(pieces) - 1
+        stage2(LAST, 0)
+        stage2(LAST, 1)
+        empty_out(LAST, 0, "s")
+        empty_out(LAST, 1, "s")
+        store(LAST, 0)
+        centre(k, 0, P)
+        centre(k, P, 2 * P)
+        quantize_a(k, 0, P)
+        quantize_a(k, P, 2 * P)
+        stage2(LAST, 2)
+        stage2(LAST, 3)
+        empty_out(LAST, 2, "s")
+        empty_out(LAST, 3, "v")
+        store(LAST, 1)

@@ -36,8 +36,8 @@ def tile_landmark_distance_cross_covariance_s14_kernel(
         warm = keep.tile([P, 1], F32, name="warm")
         e_sb = keep.tile([P, V * H, 4], BF16, name="e_sb")
         m_sb = keep.tile([P, V * H, 4], BF16, name="m_sb")
-        c_sc_raw = keep.tile([P, V, J], U8, name="c_sc_raw", align_bytes=64)
-        c_sc = keep.tile([P, V * H, 512], U8, name="c_sc", align_bytes=64)
+        c_sc_raw = keep.tile([P, J], U8, name="c_sc_raw", align_bytes=64)
+        c_sc = [keep.tile([P, H, 512], U8, name=f"c_sc{v}", align_bytes=64) for v in range(V)]
         b_sc = keep.tile([P, V * H, R], U8, name="b_sc", align_bytes=64)
         c_raw = [keep.tile([P, 2 * J], U8, name=f"c_raw{v}", align_bytes=64) for v in range(V)]
         c_cd = [keep.tile([P, 1024], U8, name=f"c_cd{g}", align_bytes=64) for g in range(V * H)]
@@ -64,18 +64,23 @@ def tile_landmark_distance_cross_covariance_s14_kernel(
                     in_=src[:, 4 * q : 4 * q + 4, :].rearrange("g r n -> r g n").bitcast(I32),
                 )
 
-        nc.vector.memset(c_sc_raw[:].rearrange("p v n -> p (v n)").bitcast(I32), 0)
+        nc.vector.memset(c_sc_raw[:].bitcast(I32), 0)
         nc.gpsimd.memset(warm[:], 1.0)
         make_identity(nc, ident[:])
+        for v in range(1, V):
+            nc.gpsimd.memset(c_sc[v][:].rearrange("p h n -> p (h n)").bitcast(I32), 0)
         nc.gpsimd.memset(b_sc[:].rearrange("p g n -> p (g n)").bitcast(I32), 0)
         e_rows = e.rearrange("v j -> (v j)").rearrange("(g p t) -> p g t", p=P, t=4)
         m_rows = m.rearrange("v j -> (v j)").rearrange("(g p t) -> p g t", p=P, t=4)
         nc.scalar.dma_start(out=e_sb[:, :2, :], in_=e_rows[:, :2, :])
         nc.scalar.activation(out=warm[:], in_=warm[:], func=SQRT)
 
-        load_c(0)
         load_x(0, 0)
-        load_scales(c_sc_raw, c_scales)
+        load_c(0)
+        for q in range(4):
+            nc.sync.dma_start(
+                out=c_sc_raw[32 * q : 32 * q + 16].bitcast(I32), in_=c_scales[:, 4 * q : 4 * q + 4, :].bitcast(I32)
+            )
         load_x(0, 1)
         nc.sync.dma_start(out=m_sb[:, :2, :], in_=m_rows[:, :2, :])
         load_x(1, 0)
@@ -89,14 +94,6 @@ def tile_landmark_distance_cross_covariance_s14_kernel(
         load_x(3, 1)
         nc.sync.dma_start(out=e_sb[:, 2:, :], in_=e_rows[:, 2:, :])
         nc.sync.dma_start(out=m_sb[:, 2:, :], in_=m_rows[:, 2:, :])
-        load_c(2)
-        load_c(3)
-        for j in range(4, V * H):
-            load_x(j, 0)
-            load_x(j, 1)
-            if j % 2 == 0:
-                load_b(j // 2 - 1)
-        load_b(3)
 
         def permute_c(g):
             v, h = g // 2, g % 2
@@ -105,12 +102,18 @@ def tile_landmark_distance_cross_covariance_s14_kernel(
                 in_=c_raw[v][:, h * 1024 : (h + 1) * 1024].rearrange("p (m t b) -> p t m b", t=4, b=2),
             )
 
-        def permute_c_scales(g):
-            v, h = g // 2, g % 2
+        def permute_c_scales(h):
             nc.vector.tensor_copy(
-                out=c_sc[:, g, :].rearrange("p (t m) -> p t m", t=4),
-                in_=c_sc_raw[:, v, h * 512 : (h + 1) * 512].rearrange("p (m t) -> p t m", t=4),
+                out=c_sc[0][:, h, :].rearrange("p (t m) -> p t m", t=4),
+                in_=c_sc_raw[:, h * 512 : (h + 1) * 512].rearrange("p (m t) -> p t m", t=4),
             )
+
+        def spread_c_scales(v):
+            for q in range(4):
+                nc.sync.dma_start(
+                    out=c_sc[v][32 * q : 32 * q + 4].rearrange("p h n -> p (h n)").bitcast(I32),
+                    in_=c_sc[0][32 * q + 4 * v : 32 * q + 4 * v + 4].rearrange("p h n -> p (h n)").bitcast(I32),
+                )
 
         banks = {}
 
@@ -162,7 +165,7 @@ def tile_landmark_distance_cross_covariance_s14_kernel(
                 nc.tensor.matmul_mx(
                     out=acc[:, : n1 - n0],
                     lhsT=c_cd[g][:, 256 * t : 256 * (t + 1)].bitcast(FP4X4),
-                    lhsT_scale=c_sc[:, g, 128 * t : 128 * (t + 1)],
+                    lhsT_scale=c_sc[j // 2][:, h, 128 * t : 128 * (t + 1)],
                     rhs=codes[:, n0:n1].bitcast(FP8X4),
                     rhs_scale=scales[:, n0:n1],
                     start=True,
@@ -189,9 +192,9 @@ def tile_landmark_distance_cross_covariance_s14_kernel(
             if a == 0:
                 cent[k] = work.tile([P, N, 4], BF16, name="cent", align_bytes=64)
             nc.vector.tensor_tensor(
-                out=cent[k][:, a:b, :].rearrange("p (c i) t -> p c t i", i=4),
-                in0=dist[k][:, :, a:b].rearrange("p t (c i) -> p c t i", i=4),
-                in1=m_sb[:, g, :].unsqueeze(1).unsqueeze(3).to_broadcast([P, (b - a) // 4, 4, 4]),
+                out=cent[k][:, a:b, :].rearrange("p (c i) t -> p c t i", i=2),
+                in0=dist[k][:, :, a:b].rearrange("p t (c i) -> p c t i", i=2),
+                in1=m_sb[:, g, :].unsqueeze(1).unsqueeze(3).to_broadcast([P, (b - a) // 2, 4, 2]),
                 op=SUB,
             )
 
@@ -254,23 +257,40 @@ def tile_landmark_distance_cross_covariance_s14_kernel(
         transpose_x(0, 0)
         transpose_x(0, 1)
         permute_c(0)
-        permute_c_scales(0)
         empty_x(0, 0, "s")
-        empty_x(0, 1, "s")
         quantize_x(0, 0, 256)
-        quantize_x(0, 256, N)
+        permute_c_scales(0)
         stage1(0)
-        permute_c(1)
+        empty_x(0, 1, "v")
         permute_c_scales(1)
+        quantize_x(0, 256, N)
+        root(0)
+        stage1(1)
+        permute_c(1)
+        for v in range(1, V):
+            spread_c_scales(v)
+        load_c(2)
+        load_c(3)
+        for j in range(4, V * H):
+            load_x(j, 0)
+            load_x(j, 1)
+            if j % 2 == 0:
+                load_b(j // 2 - 1)
+        load_b(3)
         transpose_x(1, 0)
         transpose_x(1, 1)
+        root(1)
+        empty_x(1, 0, "s")
+        centre(0, 0, 256)
+        empty_x(1, 1, "v")
+        quantize_a(0, 0, 256)
+        stage1(2)
+        transpose_x(2, 0)
+        transpose_x(2, 1)
 
-        filler = {}
-        for g in range(2, V * H):
-            filler[g - 2 if g < 4 else 2 * g - 4] = g
-
-        done = []
-        for k, (j, h, n0, n1) in enumerate(pieces):
+        for k in range(2, len(pieces)):
+            j, h, n0, n1 = pieces[k]
+            width = pieces[k - 1][3] - pieces[k - 1][2]
             pos = len([p for p in pieces[:k] if p[0] == j])
             first = pos == 0
             second = pos == (2 if j == 0 else 1)
@@ -284,41 +304,41 @@ def tile_landmark_distance_cross_covariance_s14_kernel(
             if todo:
                 stage2(todo[0], 2 * todo[1])
                 stage2(todo[0], 2 * todo[1] + 1)
-            if first and j + 2 <= LAST:
-                transpose_x(j + 2, 0)
-                transpose_x(j + 2, 1)
             root(k)
-            if k == 0:
-                empty_x(1, 0, "s")
-                empty_x(1, 1, "s")
+            oe = "s"
             if todo:
                 empty_out(todo[0], 2 * todo[1], "s")
-                empty_out(todo[0], 2 * todo[1] + 1, "s")
-                store(*todo)
-            split = not ((first and j + 1 <= LAST) or (second and j + 2 <= LAST))
-            if k >= 1:
-                w = pieces[k - 1][3] - pieces[k - 1][2]
-                if split:
-                    centre(k - 1, 0, w // 2)
-                    centre(k - 1, w // 2, w)
-                else:
-                    centre(k - 1, 0, w)
+                if oe == "s":
+                    empty_out(todo[0], 2 * todo[1] + 1, "s")
+            fill = (k == 2) or (first and j + 1 <= LAST) or (second and j + 2 <= LAST) or (todo and oe == "v")
+            if fill:
+                centre(k - 1, 0, width)
+            else:
+                centre(k - 1, 0, width // 2)
+                centre(k - 1, width // 2, width)
+            if k == 2:
+                quantize_x(1)
             if first and j + 1 <= LAST:
                 quantize_x(j + 1)
             if second and j + 2 <= LAST:
                 empty_x(j + 2, 0, "v")
                 empty_x(j + 2, 1, "s")
-            if k in filler:
-                permute_c(filler[k])
-                permute_c_scales(filler[k])
-            if k >= 1:
-                if split:
-                    quantize_a(k - 1, 0, w // 2)
-                    quantize_a(k - 1, w // 2, w)
-                else:
-                    quantize_a(k - 1, 0, w)
+            if k - 2 in (0, 1, 3, 5, 7, 9):
+                permute_c(2 + (0, 1, 3, 5, 7, 9).index(k - 2))
+            if todo:
+                if oe == "v":
+                    empty_out(todo[0], 2 * todo[1] + 1, "v")
+                store(*todo)
+            if fill:
+                quantize_a(k - 1, 0, width)
+            else:
+                quantize_a(k - 1, 0, width // 2)
+                quantize_a(k - 1, width // 2, width)
             if k + 1 < len(pieces):
                 stage1(k + 1)
+            if first and 1 <= j and j + 2 <= LAST:
+                transpose_x(j + 2, 0)
+                transpose_x(j + 2, 1)
 
         k = len(pieces) - 1
         stage2(LAST, 0)

@@ -36,21 +36,24 @@ def tile_landmark_distance_cross_covariance_s14_kernel(
         warm = keep.tile([P, 1], F32, name="warm")
         e_sb = keep.tile([P, V * H, 4], BF16, name="e_sb")
         m_sb = keep.tile([P, V * H, 4], BF16, name="m_sb")
+        m_wide = keep.tile([P, P], F32, name="m_wide")
+        m_turn = keep.tile([P, P], F32, name="m_turn")
+        m_ps = psum.tile([P, P], F32, name="m_ps", bufs=1)
         c_sc_raw = keep.tile([P, J], U8, name="c_sc_raw", align_bytes=64)
         c_sc = [keep.tile([P, H, 512], U8, name=f"c_sc{v}", align_bytes=64) for v in range(V)]
         b_sc = keep.tile([P, V * H, R], U8, name="b_sc", align_bytes=64)
         c_raw = [keep.tile([P, 2 * J], U8, name=f"c_raw{v}", align_bytes=64) for v in range(V)]
         c_cd = [keep.tile([P, 1024], U8, name=f"c_cd{g}", align_bytes=64) for g in range(V * H)]
         b_sb = [keep.tile([P, H, 2 * R], U8, name=f"b_sb{v}", align_bytes=64) for v in range(V)]
-        x_sb = [[keep.tile([P, 2, K], BF16, name=f"x{j}_{b}", align_bytes=64) for b in range(2)] for j in range(V * H)]
+        x_sb = [keep.tile([P, 4, K], BF16, name=f"x{j}", align_bytes=64) for j in range(V * H)]
 
-        def load_x(j, b):
+        def load_x(j, r0, r1):
             v, s = j // 2, j % 2
             src = x[v, s * N : (s + 1) * N, :].rearrange("(p r) k -> p r k", r=4)
-            nc.sync.dma_start(out=x_sb[j][b][:], in_=src[:, 2 * b : 2 * b + 2, :])
+            nc.sync.dma_start(out=x_sb[j][:, r0:r1, :], in_=src[:, r0:r1, :])
 
-        def load_c(v):
-            nc.sync.dma_start(out=c_raw[v][:].bitcast(I32), in_=c_words[v].bitcast(I32))
+        def load_c(v, b0=0, b1=2 * J):
+            nc.sync.dma_start(out=c_raw[v][:, b0:b1].bitcast(I32), in_=c_words[v, :, b0:b1].bitcast(I32))
 
         def load_b(v):
             nc.sync.dma_start(
@@ -72,28 +75,27 @@ def tile_landmark_distance_cross_covariance_s14_kernel(
         nc.gpsimd.memset(b_sc[:].rearrange("p g n -> p (g n)").bitcast(I32), 0)
         e_rows = e.rearrange("v j -> (v j)").rearrange("(g p t) -> p g t", p=P, t=4)
         m_rows = m.rearrange("v j -> (v j)").rearrange("(g p t) -> p g t", p=P, t=4)
-        nc.scalar.dma_start(out=e_sb[:, :2, :], in_=e_rows[:, :2, :])
+        nc.scalar.dma_start(out=e_sb[:, :4, :], in_=e_rows[:, :4, :])
         nc.scalar.activation(out=warm[:], in_=warm[:], func=SQRT)
+        nc.gpsimd.memset(m_wide[:], 0.0)
 
-        load_x(0, 0)
+        load_x(0, 0, 2)
         load_c(0)
         for q in range(4):
             nc.sync.dma_start(
                 out=c_sc_raw[32 * q : 32 * q + 16].bitcast(I32), in_=c_scales[:, 4 * q : 4 * q + 4, :].bitcast(I32)
             )
-        load_x(0, 1)
-        nc.sync.dma_start(out=m_sb[:, :2, :], in_=m_rows[:, :2, :])
-        load_x(1, 0)
-        load_x(1, 1)
+        load_x(0, 2, 4)
+        nc.sync.dma_start(out=m_sb[:, :4, :], in_=m_rows[:, :4, :])
+        load_x(1, 0, 4)
+        nc.sync.dma_start(out=m_sb[:, 4:, :], in_=m_rows[:, 4:, :])
+        nc.sync.dma_start(out=e_sb[:, 4:, :], in_=e_rows[:, 4:, :])
+        nc.gpsimd.tensor_copy(out=m_wide[:, :32], in_=m_sb[:].rearrange("p g t -> p (g t)"))
         load_c(1)
-        load_x(2, 0)
-        load_x(2, 1)
+        load_x(2, 0, 4)
         load_b(0)
         load_scales(b_sc, b_scales)
-        load_x(3, 0)
-        load_x(3, 1)
-        nc.sync.dma_start(out=e_sb[:, 2:, :], in_=e_rows[:, 2:, :])
-        nc.sync.dma_start(out=m_sb[:, 2:, :], in_=m_rows[:, 2:, :])
+        load_x(3, 0, 4)
 
         def permute_c(g):
             v, h = g // 2, g % 2
@@ -117,23 +119,25 @@ def tile_landmark_distance_cross_covariance_s14_kernel(
 
         banks = {}
 
-        def transpose_x(j, b):
+        def transpose_x(j, r0, r1):
             xp = psum.tile([P, 2, 2, P], F32, name="xp", bufs=2)
-            words = x_sb[j][b][:].rearrange("p r k -> p (r k)").bitcast(F32)
-            for rr in range(2):
+            words = x_sb[j][:].rearrange("p r k -> p (r k)").bitcast(F32)
+            for r in range(r0, r1):
                 for u in range(2):
-                    nc.tensor.transpose(xp[:, rr, u, :], words[:, 256 * rr + u : 256 * (rr + 1) : 2], ident[:])
-            banks[j, b] = xp
+                    nc.tensor.transpose(
+                        xp[:, r - r0, u, :], words[:, 256 * r + u : 256 * (r + 1) : 2], ident[:]
+                    )
+            banks[j, r0] = xp
 
         grouped = {}
         xq = {}
 
-        def empty_x(j, b, eng):
+        def empty_x(j, r0, r1, eng):
             if j not in grouped:
                 grouped[j] = work.tile([P, N, 4], BF16, name="grouped", align_bytes=64)
-            dst = grouped[j][:].rearrange("p n t -> p (n t)").bitcast(F32)[:, b * 512 : (b + 1) * 512]
-            dst = dst.rearrange("p (r s u) -> p r s u", r=2, u=2)
-            src = banks[j, b][:].rearrange("p r u s -> p r s u")
+            dst = grouped[j][:].rearrange("p n t -> p (n t)").bitcast(F32)[:, r0 * 256 : r1 * 256]
+            dst = dst.rearrange("p (r w u) -> p r w u", w=P, u=2)
+            src = banks[j, r0][:, : r1 - r0].rearrange("p r u w -> p r w u")
             if eng == "v":
                 nc.vector.tensor_copy(out=dst, in_=src)
             else:
@@ -156,12 +160,12 @@ def tile_landmark_distance_cross_covariance_s14_kernel(
         cent = {}
         aq = {}
 
-        def stage1(k):
+        def stage1(k, t0=0, t1=4):
             j, h, n0, n1 = pieces[k]
             g = (j // 2) * 2 + h
             codes, scales = xq[j]
-            for t in range(4):
-                acc = psum.tile([P, N], F32, name="gram", bufs=4)
+            for t in range(t0, t1):
+                acc = psum.tile([P, N], F32, name="gram", bufs=3)
                 nc.tensor.matmul_mx(
                     out=acc[:, : n1 - n0],
                     lhsT=c_cd[g][:, 256 * t : 256 * (t + 1)].bitcast(FP4X4),
@@ -173,11 +177,12 @@ def tile_landmark_distance_cross_covariance_s14_kernel(
                 )
                 gram[k, t] = acc
 
-        def root(k):
+        def root(k, t0=0, t1=4):
             j, h, n0, n1 = pieces[k]
             g = (j // 2) * 2 + h
-            dist[k] = work.tile([P, 4, N], F32, name="dist", bufs=3)
-            for t in range(4):
+            if t0 == 0:
+                dist[k] = work.tile([P, 4, N], F32, name="dist", bufs=3)
+            for t in range(t0, t1):
                 nc.scalar.activation(
                     out=dist[k][:, t, : n1 - n0],
                     in_=gram[k, t][:, : n1 - n0],
@@ -190,11 +195,21 @@ def tile_landmark_distance_cross_covariance_s14_kernel(
             j, h, n0, n1 = pieces[k]
             g = (j // 2) * 2 + h
             if a == 0:
-                cent[k] = work.tile([P, N, 4], BF16, name="cent", align_bytes=64)
+                cent[k] = work.tile([P, N, 4], BF16, name="cent", align_bytes=64, bufs=1)
+            cut = a + (b - a) * 3 // 4 if k >= 3 else b
+            if cut < b:
+                w = (b - cut) // 1
+                for q in range(cut, b, w):
+                    nc.gpsimd.tensor_tensor(
+                        out=cent[k][:, q : q + w, :],
+                        in0=dist[k][:, :, q : q + w].rearrange("p t n -> p n t"),
+                        in1=m_sb[:, g, :].unsqueeze(1).to_broadcast([P, w, 4]),
+                        op=SUB,
+                    )
             nc.vector.tensor_tensor(
-                out=cent[k][:, a:b, :].rearrange("p (c i) t -> p c t i", i=2),
-                in0=dist[k][:, :, a:b].rearrange("p t (c i) -> p c t i", i=2),
-                in1=m_sb[:, g, :].unsqueeze(1).unsqueeze(3).to_broadcast([P, (b - a) // 2, 4, 2]),
+                out=cent[k][:, a:cut, :].rearrange("p (c i) t -> p c t i", i=2),
+                in0=dist[k][:, :, a:cut].rearrange("p t (c i) -> p c t i", i=2),
+                in1=(m_sb[:, g, :] if k < 3 else m_ps[:, 4 * g : 4 * g + 4]).unsqueeze(1).unsqueeze(3).to_broadcast([P, (cut - a) // 2, 4, 2]),
                 op=SUB,
             )
 
@@ -254,39 +269,41 @@ def tile_landmark_distance_cross_covariance_s14_kernel(
             else:
                 pieces += [(j, 0, 0, N), (j, 1, 0, N)]
 
-        transpose_x(0, 0)
-        transpose_x(0, 1)
+        transpose_x(0, 0, 2)
+        transpose_x(0, 2, 4)
         permute_c(0)
-        empty_x(0, 0, "s")
+        empty_x(0, 0, 2, "s")
         quantize_x(0, 0, 256)
         permute_c_scales(0)
-        stage1(0)
-        empty_x(0, 1, "v")
+        stage1(0, 0, 3)
+        empty_x(0, 2, 4, "v")
         permute_c_scales(1)
         quantize_x(0, 256, N)
+        stage1(0, 3, 4)
         root(0)
-        stage1(1)
+        stage1(1, 0, 3)
         permute_c(1)
         for v in range(1, V):
             spread_c_scales(v)
         load_c(2)
         load_c(3)
         for j in range(4, V * H):
-            load_x(j, 0)
-            load_x(j, 1)
+            load_x(j, 0, 4)
             if j % 2 == 0:
                 load_b(j // 2 - 1)
         load_b(3)
-        transpose_x(1, 0)
-        transpose_x(1, 1)
+        stage1(1, 3, 4)
         root(1)
-        empty_x(1, 0, "s")
+        stage1(2, 0, 1)
+        transpose_x(1, 0, 2)
+        transpose_x(1, 2, 4)
+        stage1(2, 1, 3)
         centre(0, 0, 256)
-        empty_x(1, 1, "v")
+        root(2, 0, 1)
+        empty_x(1, 0, 2, "s")
+        empty_x(1, 2, 4, "v")
         quantize_a(0, 0, 256)
-        stage1(2)
-        transpose_x(2, 0)
-        transpose_x(2, 1)
+        quantize_x(1)
 
         for k in range(2, len(pieces)):
             j, h, n0, n1 = pieces[k]
@@ -301,44 +318,42 @@ def tile_landmark_distance_cross_covariance_s14_kernel(
                 todo = (j - 2, 1)
             elif j == LAST and pos == 2:
                 todo = (j - 1, 1)
+            oe = "s"
+            stage1(k, 3, 4)
             if todo:
                 stage2(todo[0], 2 * todo[1])
                 stage2(todo[0], 2 * todo[1] + 1)
-            root(k)
-            oe = "s"
+            root(k, 1 if k == 2 else 0)
+            if k == 3:
+                m_t = psum.tile([P, P], F32, name="xp", bufs=2)
+                nc.tensor.transpose(m_t[:], m_wide[:], ident[:])
+                nc.scalar.copy(out=m_turn[:], in_=m_t[:])
+            if k + 1 < len(pieces):
+                stage1(k + 1, 0, 2)
+            if (first and 1 <= j and j + 2 <= LAST) or k == 2:
+                transpose_x(j + 2, 0, 2)
+                transpose_x(j + 2, 2, 4)
+            if k + 1 < len(pieces):
+                stage1(k + 1, 2, 3)
+            if k == 3:
+                nc.tensor.transpose(m_ps[:], m_turn[:], ident[:])
             if todo:
                 empty_out(todo[0], 2 * todo[1], "s")
                 if oe == "s":
                     empty_out(todo[0], 2 * todo[1] + 1, "s")
-            fill = (k == 2) or (first and j + 1 <= LAST) or (second and j + 2 <= LAST) or (todo and oe == "v")
-            if fill:
-                centre(k - 1, 0, width)
-            else:
-                centre(k - 1, 0, width // 2)
-                centre(k - 1, width // 2, width)
-            if k == 2:
-                quantize_x(1)
+            centre(k - 1, 0, width)
             if first and j + 1 <= LAST:
                 quantize_x(j + 1)
             if second and j + 2 <= LAST:
-                empty_x(j + 2, 0, "v")
-                empty_x(j + 2, 1, "s")
-            if k - 2 in (0, 1, 3, 5, 7, 9):
-                permute_c(2 + (0, 1, 3, 5, 7, 9).index(k - 2))
+                empty_x(j + 2, 0, 2, "v")
+                empty_x(j + 2, 2, 4, "v")
+            if k - 2 in (1, 2, 4, 6, 8, 10):
+                permute_c(2 + (1, 2, 4, 6, 8, 10).index(k - 2))
             if todo:
                 if oe == "v":
                     empty_out(todo[0], 2 * todo[1] + 1, "v")
                 store(*todo)
-            if fill:
-                quantize_a(k - 1, 0, width)
-            else:
-                quantize_a(k - 1, 0, width // 2)
-                quantize_a(k - 1, width // 2, width)
-            if k + 1 < len(pieces):
-                stage1(k + 1)
-            if first and 1 <= j and j + 2 <= LAST:
-                transpose_x(j + 2, 0)
-                transpose_x(j + 2, 1)
+            quantize_a(k - 1, 0, width)
 
         k = len(pieces) - 1
         stage2(LAST, 0)
@@ -346,8 +361,7 @@ def tile_landmark_distance_cross_covariance_s14_kernel(
         empty_out(LAST, 0, "s")
         empty_out(LAST, 1, "s")
         store(LAST, 0)
-        centre(k, 0, P)
-        centre(k, P, 2 * P)
+        centre(k, 0, 256)
         quantize_a(k, 0, P)
         quantize_a(k, P, 2 * P)
         stage2(LAST, 2)

@@ -11,13 +11,16 @@ U8 = mybir.dt.uint8
 FP8X4 = mybir.dt.float8_e4m3fn_x4
 FP4X4 = mybir.dt.float4_e2m1fn_x4
 SQRT = mybir.ActivationFunctionType.Sqrt
-SUB = mybir.AluOpType.subtract
+SUBTRACT = mybir.AluOpType.subtract
 
 V, M, K, J, R = 4, 1024, 512, 1024, 512
 P = 128
-H = 2
-N = 512
-UNITS = V * H * H
+PACK = 4
+N = P * PACK
+HALVES = V * M // N
+GROUPS = V * J // N
+LAST = HALVES - 1
+Q_ROWS = 4
 
 FLOPS = 2 * V * M * J * (K + R)
 
@@ -34,38 +37,48 @@ def tile_landmark_distance_cross_covariance_s14_kernel(
 
         ident = keep.tile([P, P], F32, name="ident")
         warm = keep.tile([P, 1], F32, name="warm")
-        e_sb = keep.tile([P, V * H, 4], BF16, name="e_sb")
-        m_sb = keep.tile([P, V * H, 4], BF16, name="m_sb")
-        m_wide = keep.tile([P, P], F32, name="m_wide")
-        m_turn = keep.tile([P, P], F32, name="m_turn")
-        m_ps = psum.tile([P, P], F32, name="m_ps", bufs=1)
+        e_sb = keep.tile([P, GROUPS, PACK], BF16, name="e_sb")
+        m_sb = keep.tile([P, GROUPS, PACK], BF16, name="m_sb")
         c_sc_raw = keep.tile([P, J], U8, name="c_sc_raw", align_bytes=64)
-        c_sc = [keep.tile([P, H, 512], U8, name=f"c_sc{v}", align_bytes=64) for v in range(V)]
-        b_sc = keep.tile([P, V * H, R], U8, name="b_sc", align_bytes=64)
+        c_sc = [keep.tile([P, 2, N], U8, name=f"c_sc{v}", align_bytes=64) for v in range(V)]
+        b_sc = keep.tile([P, GROUPS, R], U8, name="b_sc", align_bytes=64)
         c_raw = [keep.tile([P, 2 * J], U8, name=f"c_raw{v}", align_bytes=64) for v in range(V)]
-        c_cd = [keep.tile([P, 1024], U8, name=f"c_cd{g}", align_bytes=64) for g in range(V * H)]
-        b_sb = [keep.tile([P, H, 2 * R], U8, name=f"b_sb{v}", align_bytes=64) for v in range(V)]
-        x_sb = [keep.tile([P, 4, K], BF16, name=f"x{j}", align_bytes=64) for j in range(V * H)]
+        c_codes = [keep.tile([P, 2 * N], U8, name=f"c_codes{g}", align_bytes=64) for g in range(GROUPS)]
+        b_codes = [keep.tile([P, 2, 2 * R], U8, name=f"b_codes{v}", align_bytes=64) for v in range(V)]
+        x_sb = [keep.tile([P, 4, K], BF16, name=f"x{hv}", align_bytes=64) for hv in range(HALVES)]
 
-        def load_x(j, r0, r1):
-            v, s = j // 2, j % 2
-            src = x[v, s * N : (s + 1) * N, :].rearrange("(p r) k -> p r k", r=4)
-            nc.sync.dma_start(out=x_sb[j][:, r0:r1, :], in_=src[:, r0:r1, :])
+        def samples(tensor, hv):
+            first = hv % 2 * N
+            return tensor[hv // 2, first : first + N, :].rearrange("(p r) k -> p r k", r=4)
 
-        def load_c(v, b0=0, b1=2 * J):
+        def load_x(hv, r0, r1):
+            nc.sync.dma_start(out=x_sb[hv][:, r0:r1, :], in_=samples(x, hv)[:, r0:r1, :])
+
+        def load_c(v, b0, b1):
             nc.sync.dma_start(out=c_raw[v][:, b0:b1].bitcast(I32), in_=c_words[v, :, b0:b1].bitcast(I32))
+
+        def load_c_scales():
+            for q in range(4):
+                nc.sync.dma_start(
+                    out=c_sc_raw[32 * q : 32 * q + Q_ROWS * V].bitcast(I32),
+                    in_=c_scales[:, Q_ROWS * q : Q_ROWS * (q + 1), :].bitcast(I32),
+                )
 
         def load_b(v):
             nc.sync.dma_start(
-                out=b_sb[v][:].bitcast(I32), in_=b_words[2 * v : 2 * v + 2].rearrange("g p n -> p g n").bitcast(I32)
+                out=b_codes[v][:].bitcast(I32),
+                in_=b_words[2 * v : 2 * v + 2].rearrange("g p n -> p g n").bitcast(I32),
             )
 
-        def load_scales(plane, src):
+        def load_b_scales():
             for q in range(4):
                 nc.sync.dma_start(
-                    out=plane[32 * q : 32 * q + 4].bitcast(I32),
-                    in_=src[:, 4 * q : 4 * q + 4, :].rearrange("g r n -> r g n").bitcast(I32),
+                    out=b_sc[32 * q : 32 * q + Q_ROWS].bitcast(I32),
+                    in_=b_scales[:, Q_ROWS * q : Q_ROWS * (q + 1), :].rearrange("g r n -> r g n").bitcast(I32),
                 )
+
+        e_rows = e.rearrange("v j -> (v j)").rearrange("(g p t) -> p g t", p=P, t=PACK)
+        m_rows = m.rearrange("v j -> (v j)").rearrange("(g p t) -> p g t", p=P, t=PACK)
 
         nc.vector.memset(c_sc_raw[:].bitcast(I32), 0)
         nc.gpsimd.memset(warm[:], 1.0)
@@ -73,299 +86,265 @@ def tile_landmark_distance_cross_covariance_s14_kernel(
         for v in range(1, V):
             nc.gpsimd.memset(c_sc[v][:].rearrange("p h n -> p (h n)").bitcast(I32), 0)
         nc.gpsimd.memset(b_sc[:].rearrange("p g n -> p (g n)").bitcast(I32), 0)
-        e_rows = e.rearrange("v j -> (v j)").rearrange("(g p t) -> p g t", p=P, t=4)
-        m_rows = m.rearrange("v j -> (v j)").rearrange("(g p t) -> p g t", p=P, t=4)
+
         nc.scalar.dma_start(out=e_sb[:, :4, :], in_=e_rows[:, :4, :])
         nc.scalar.activation(out=warm[:], in_=warm[:], func=SQRT)
-        nc.gpsimd.memset(m_wide[:], 0.0)
 
         load_x(0, 0, 2)
-        load_c(0)
-        for q in range(4):
-            nc.sync.dma_start(
-                out=c_sc_raw[32 * q : 32 * q + 16].bitcast(I32), in_=c_scales[:, 4 * q : 4 * q + 4, :].bitcast(I32)
-            )
+        load_c(0, 0, J)
+        load_c_scales()
         load_x(0, 2, 4)
+        load_c(0, J, 2 * J)
         nc.sync.dma_start(out=m_sb[:, :4, :], in_=m_rows[:, :4, :])
         load_x(1, 0, 4)
-        nc.sync.dma_start(out=m_sb[:, 4:, :], in_=m_rows[:, 4:, :])
-        nc.sync.dma_start(out=e_sb[:, 4:, :], in_=e_rows[:, 4:, :])
-        nc.gpsimd.tensor_copy(out=m_wide[:, :32], in_=m_sb[:].rearrange("p g t -> p (g t)"))
-        load_c(1)
+        load_c(1, 0, 2 * J)
         load_x(2, 0, 4)
         load_b(0)
-        load_scales(b_sc, b_scales)
+        load_b_scales()
         load_x(3, 0, 4)
+        nc.sync.dma_start(out=m_sb[:, 4:, :], in_=m_rows[:, 4:, :])
+        nc.sync.dma_start(out=e_sb[:, 4:, :], in_=e_rows[:, 4:, :])
 
         def permute_c(g):
-            v, h = g // 2, g % 2
+            raw = c_raw[g // 2][:, g % 2 * 2 * N : (g % 2 + 1) * 2 * N]
             nc.vector.tensor_copy(
-                out=c_cd[g][:].rearrange("p (t m b) -> p t m b", t=4, b=2),
-                in_=c_raw[v][:, h * 1024 : (h + 1) * 1024].rearrange("p (m t b) -> p t m b", t=4, b=2),
+                out=c_codes[g][:].rearrange("p (t s b) -> p t s b", t=PACK, b=2),
+                in_=raw.rearrange("p (s t b) -> p t s b", t=PACK, b=2),
             )
 
         def permute_c_scales(h):
             nc.vector.tensor_copy(
-                out=c_sc[0][:, h, :].rearrange("p (t m) -> p t m", t=4),
-                in_=c_sc_raw[:, h * 512 : (h + 1) * 512].rearrange("p (m t) -> p t m", t=4),
+                out=c_sc[0][:, h, :].rearrange("p (t s) -> p t s", t=PACK),
+                in_=c_sc_raw[:, h * N : (h + 1) * N].rearrange("p (s t) -> p t s", t=PACK),
             )
 
         def spread_c_scales(v):
             for q in range(4):
+                row = 32 * q + Q_ROWS * v
                 nc.sync.dma_start(
-                    out=c_sc[v][32 * q : 32 * q + 4].rearrange("p h n -> p (h n)").bitcast(I32),
-                    in_=c_sc[0][32 * q + 4 * v : 32 * q + 4 * v + 4].rearrange("p h n -> p (h n)").bitcast(I32),
+                    out=c_sc[v][32 * q : 32 * q + Q_ROWS].rearrange("p h n -> p (h n)").bitcast(I32),
+                    in_=c_sc[0][row : row + Q_ROWS].rearrange("p h n -> p (h n)").bitcast(I32),
                 )
 
-        banks = {}
-
-        def transpose_x(j, r0, r1):
-            xp = psum.tile([P, 2, 2, P], F32, name="xp", bufs=2)
-            words = x_sb[j][:].rearrange("p r k -> p (r k)").bitcast(F32)
-            for r in range(r0, r1):
-                for u in range(2):
-                    nc.tensor.transpose(
-                        xp[:, r - r0, u, :], words[:, 256 * r + u : 256 * (r + 1) : 2], ident[:]
-                    )
-            banks[j, r0] = xp
-
+        turned = {}
         grouped = {}
-        xq = {}
+        x_mx = {}
 
-        def empty_x(j, r0, r1, eng):
-            if j not in grouped:
-                grouped[j] = work.tile([P, N, 4], BF16, name="grouped", align_bytes=64)
-            dst = grouped[j][:].rearrange("p n t -> p (n t)").bitcast(F32)[:, r0 * 256 : r1 * 256]
-            dst = dst.rearrange("p (r w u) -> p r w u", w=P, u=2)
-            src = banks[j, r0][:, : r1 - r0].rearrange("p r u w -> p r w u")
-            if eng == "v":
-                nc.vector.tensor_copy(out=dst, in_=src)
-            else:
-                nc.scalar.copy(out=dst, in_=src)
+        def turn_x(hv, r0):
+            xt = psum.tile([P, 2, 2, P], F32, name="xt", bufs=2)
+            words = x_sb[hv][:].rearrange("p r k -> p (r k)").bitcast(F32)
+            for r in range(2):
+                start = (r0 + r) * K // 2
+                for u in range(2):
+                    nc.tensor.transpose(xt[:, r, u, :], words[:, start + u : start + K // 2 : 2], ident[:])
+            turned[hv, r0] = xt
 
-        def quantize_x(j, n0=0, n1=N):
-            if n0 == 0:
-                codes = work.tile([P, N], U32, name="xq", align_bytes=64)
-                scales = work.tile([P, N], U8, name="xqs", align_bytes=64)
-                xq[j] = (codes, scales)
-            codes, scales = xq[j]
+        def empty_x(hv, r0, copy):
+            if hv not in grouped:
+                grouped[hv] = work.tile([P, N, PACK], BF16, name="grouped", align_bytes=64)
+            words = grouped[hv][:].rearrange("p n t -> p (n t)").bitcast(F32)
+            words = words[:, r0 * 2 * P : (r0 + 2) * 2 * P].rearrange("p (r w u) -> p r w u", w=P, u=2)
+            copy(out=words, in_=turned[hv, r0][:].rearrange("p r u w -> p r w u"))
+
+        def quantize_x(hv, n0, n1):
+            if hv not in x_mx:
+                codes = work.tile([P, N], U32, name="x_codes", align_bytes=64)
+                scales = work.tile([P, N], U8, name="x_scales", align_bytes=64)
+                x_mx[hv] = (codes, scales)
+            codes, scales = x_mx[hv]
             nc.vector.quantize_mx(
                 out=codes[:, n0:n1].bitcast(FP8X4),
                 scales=scales[:, n0:n1],
-                in_=grouped[j][:, n0:n1, :].rearrange("p n t -> p (n t)"),
+                in_=grouped[hv][:, n0:n1, :].rearrange("p n t -> p (n t)"),
             )
+
+        pieces = [(0, 0, 0, N // 2), (0, 0, N // 2, N), (0, 1, 0, N)]
+        for hv in range(1, LAST):
+            pieces += [(hv, 0, 0, N), (hv, 1, 0, N)]
+        pieces += [(LAST, h, n0, n0 + N // 2) for n0 in (0, N // 2) for h in (0, 1)]
 
         gram = {}
         dist = {}
-        cent = {}
-        aq = {}
+        centred = {}
+        a_mx = {}
 
-        def stage1(k, t0=0, t1=4):
-            j, h, n0, n1 = pieces[k]
-            g = (j // 2) * 2 + h
-            codes, scales = xq[j]
+        def group(k):
+            hv, h, n0, n1 = pieces[k]
+            return hv // 2 * 2 + h
+
+        def first_product(k, t0, t1):
+            hv, h, n0, n1 = pieces[k]
+            codes, scales = x_mx[hv]
             for t in range(t0, t1):
-                acc = psum.tile([P, N], F32, name="gram", bufs=3)
+                gram[k, t] = psum.tile([P, N], F32, name="gram", bufs=4)
                 nc.tensor.matmul_mx(
-                    out=acc[:, : n1 - n0],
-                    lhsT=c_cd[g][:, 256 * t : 256 * (t + 1)].bitcast(FP4X4),
-                    lhsT_scale=c_sc[j // 2][:, h, 128 * t : 128 * (t + 1)],
+                    out=gram[k, t][:, : n1 - n0],
+                    lhsT=c_codes[group(k)][:, 2 * P * t : 2 * P * (t + 1)].bitcast(FP4X4),
+                    lhsT_scale=c_sc[hv // 2][:, h, P * t : P * (t + 1)],
                     rhs=codes[:, n0:n1].bitcast(FP8X4),
                     rhs_scale=scales[:, n0:n1],
                     start=True,
                     stop=True,
                 )
-                gram[k, t] = acc
 
-        def root(k, t0=0, t1=4):
-            j, h, n0, n1 = pieces[k]
-            g = (j // 2) * 2 + h
-            if t0 == 0:
-                dist[k] = work.tile([P, 4, N], F32, name="dist", bufs=3)
+        def root(k, t0, t1):
+            hv, h, n0, n1 = pieces[k]
+            if k not in dist:
+                dist[k] = work.tile([P, PACK, N], F32, name="dist", bufs=3)
             for t in range(t0, t1):
                 nc.scalar.activation(
                     out=dist[k][:, t, : n1 - n0],
                     in_=gram[k, t][:, : n1 - n0],
                     func=SQRT,
-                    bias=e_sb[:, g, t : t + 1],
+                    bias=e_sb[:, group(k), t : t + 1],
                     scale=-1.0,
                 )
 
         def centre(k, a, b):
-            j, h, n0, n1 = pieces[k]
-            g = (j // 2) * 2 + h
-            if a == 0:
-                cent[k] = work.tile([P, N, 4], BF16, name="cent", align_bytes=64, bufs=1)
-            cut = a + (b - a) * 3 // 4 if k >= 3 else b
-            if cut < b:
-                w = (b - cut) // 1
-                for q in range(cut, b, w):
-                    nc.gpsimd.tensor_tensor(
-                        out=cent[k][:, q : q + w, :],
-                        in0=dist[k][:, :, q : q + w].rearrange("p t n -> p n t"),
-                        in1=m_sb[:, g, :].unsqueeze(1).to_broadcast([P, w, 4]),
-                        op=SUB,
-                    )
+            if k not in centred:
+                centred[k] = work.tile([P, N, PACK], BF16, name="centred", align_bytes=64)
+            means = m_sb[:, group(k), :].unsqueeze(1).unsqueeze(3)
             nc.vector.tensor_tensor(
-                out=cent[k][:, a:cut, :].rearrange("p (c i) t -> p c t i", i=2),
-                in0=dist[k][:, :, a:cut].rearrange("p t (c i) -> p c t i", i=2),
-                in1=(m_sb[:, g, :] if k < 3 else m_ps[:, 4 * g : 4 * g + 4]).unsqueeze(1).unsqueeze(3).to_broadcast([P, (cut - a) // 2, 4, 2]),
-                op=SUB,
+                out=centred[k][:, a:b, :].rearrange("p (c i) t -> p c t i", i=2),
+                in0=dist[k][:, :, a:b].rearrange("p t (c i) -> p c t i", i=2),
+                in1=means.to_broadcast([P, (b - a) // 2, PACK, 2]),
+                op=SUBTRACT,
             )
 
         def quantize_a(k, a, b):
-            j, h, n0, n1 = pieces[k]
-            if (j, h) not in aq:
-                codes = work.tile([P, N], U32, name="aq", align_bytes=64, bufs=6)
-                scales = work.tile([P, N], U8, name="aqs", align_bytes=64, bufs=6)
-                aq[j, h] = (codes, scales)
-            codes, scales = aq[j, h]
+            hv, h, n0, n1 = pieces[k]
+            if (hv, h) not in a_mx:
+                codes = work.tile([P, N], U32, name="a_codes", align_bytes=64, bufs=6)
+                scales = work.tile([P, N], U8, name="a_scales", align_bytes=64, bufs=6)
+                a_mx[hv, h] = (codes, scales)
+            codes, scales = a_mx[hv, h]
             nc.vector.quantize_mx(
                 out=codes[:, n0 + a : n0 + b].bitcast(FP8X4),
                 scales=scales[:, n0 + a : n0 + b],
-                in_=cent[k][:, a:b, :].rearrange("p n t -> p (n t)"),
+                in_=centred[k][:, a:b, :].rearrange("p n t -> p (n t)"),
             )
 
         cov = {}
         rows = {}
 
-        def stage2(j, r, name="cov", bufs=2):
-            acc = psum.tile([P, R], F32, name=name, bufs=bufs)
-            v = j // 2
-            for h in range(H):
-                codes, scales = aq[j, h]
+        def second_product(hv, r, name, bufs):
+            cov[hv, r] = psum.tile([P, R], F32, name=name, bufs=bufs)
+            for h in range(2):
+                codes, scales = a_mx[hv, h]
                 nc.tensor.matmul_mx(
-                    out=acc[:],
+                    out=cov[hv, r][:],
                     lhsT=codes[:, P * r : P * (r + 1)].bitcast(FP8X4),
                     lhsT_scale=scales[:, P * r : P * (r + 1)],
-                    rhs=b_sb[v][:, h, :].bitcast(FP4X4),
-                    rhs_scale=b_sc[:, 2 * v + h, :],
+                    rhs=b_codes[hv // 2][:, h, :].bitcast(FP4X4),
+                    rhs_scale=b_sc[:, hv // 2 * 2 + h, :],
                     start=(h == 0),
-                    stop=(h == H - 1),
+                    stop=(h == 1),
                 )
-            cov[j, r] = acc
 
-        def empty_out(j, r, eng):
-            if (j, r // 2) not in rows:
-                rows[j, r // 2] = work.tile([P, 2, R], F32, name="rows", bufs=4)
-            dst = rows[j, r // 2][:, r % 2, :]
-            if eng == "v":
-                nc.vector.tensor_copy(out=dst, in_=cov[j, r][:])
-            else:
-                nc.scalar.copy(out=dst, in_=cov[j, r][:])
+        def empty_out(hv, r):
+            if (hv, r // 2) not in rows:
+                rows[hv, r // 2] = work.tile([P, 2, R], F32, name="rows", bufs=4)
+            nc.scalar.copy(out=rows[hv, r // 2][:, r % 2, :], in_=cov[hv, r][:])
 
-        def store(j, b):
-            v, s = j // 2, j % 2
-            dst = out[v, s * N : (s + 1) * N, :].rearrange("(p r) c -> p r c", r=4)
-            nc.sync.dma_start(out=dst[:, 2 * b : 2 * b + 2, :], in_=rows[j, b][:])
+        def store(hv, r0, r1):
+            part = rows[hv, r0 // 2][:, r0 % 2 : r0 % 2 + r1 - r0, :]
+            nc.sync.dma_start(out=samples(out, hv)[:, r0:r1, :], in_=part)
 
-        LAST = V * H - 1
-        pieces = []
-        for j in range(V * H):
-            if j == 0:
-                pieces += [(0, 0, 0, 256), (0, 0, 256, N), (0, 1, 0, N)]
-            elif j == LAST:
-                pieces += [(j, 0, 0, 256), (j, 1, 0, 256), (j, 0, 256, N), (j, 1, 256, N)]
-            else:
-                pieces += [(j, 0, 0, N), (j, 1, 0, N)]
+        on_vector = nc.vector.tensor_copy
+        on_scalar = nc.scalar.copy
 
-        transpose_x(0, 0, 2)
-        transpose_x(0, 2, 4)
+        turn_x(0, 0)
+        turn_x(0, 2)
         permute_c(0)
-        empty_x(0, 0, 2, "s")
-        quantize_x(0, 0, 256)
         permute_c_scales(0)
-        stage1(0, 0, 3)
-        empty_x(0, 2, 4, "v")
+        empty_x(0, 0, on_scalar)
+        quantize_x(0, 0, N // 2)
+        first_product(0, 0, 4)
+        root(0, 0, 4)
+        empty_x(0, 2, on_vector)
         permute_c_scales(1)
-        quantize_x(0, 256, N)
-        stage1(0, 3, 4)
-        root(0)
-        stage1(1, 0, 3)
+        quantize_x(0, N // 2, N)
         permute_c(1)
+        first_product(1, 0, 4)
         for v in range(1, V):
             spread_c_scales(v)
-        load_c(2)
-        load_c(3)
-        for j in range(4, V * H):
-            load_x(j, 0, 4)
-            if j % 2 == 0:
-                load_b(j // 2 - 1)
+        load_c(2, 0, 2 * J)
+        load_c(3, 0, 2 * J)
+        for hv in range(4, HALVES):
+            load_x(hv, 0, 4)
+            if hv % 2 == 0:
+                load_b(hv // 2 - 1)
         load_b(3)
-        stage1(1, 3, 4)
-        root(1)
-        stage1(2, 0, 1)
-        transpose_x(1, 0, 2)
-        transpose_x(1, 2, 4)
-        stage1(2, 1, 3)
-        centre(0, 0, 256)
+        root(1, 0, 4)
+        first_product(2, 0, 1)
+        turn_x(1, 0)
+        turn_x(1, 2)
+        first_product(2, 1, 4)
+        centre(0, 0, N // 2)
         root(2, 0, 1)
-        empty_x(1, 0, 2, "s")
-        empty_x(1, 2, 4, "v")
-        quantize_a(0, 0, 256)
-        quantize_x(1)
+        empty_x(1, 0, on_vector)
+        empty_x(1, 2, on_scalar)
+        quantize_a(0, 0, N // 2)
+        quantize_x(1, 0, N)
 
         for k in range(2, len(pieces)):
-            j, h, n0, n1 = pieces[k]
-            width = pieces[k - 1][3] - pieces[k - 1][2]
-            pos = len([p for p in pieces[:k] if p[0] == j])
-            first = pos == 0
-            second = pos == (2 if j == 0 else 1)
-            todo = None
-            if second and j >= 1:
-                todo = (j - 1, 0)
-            elif first and j >= 2:
-                todo = (j - 2, 1)
-            elif j == LAST and pos == 2:
-                todo = (j - 1, 1)
-            oe = "s"
-            stage1(k, 3, 4)
-            if todo:
-                stage2(todo[0], 2 * todo[1])
-                stage2(todo[0], 2 * todo[1] + 1)
-            root(k, 1 if k == 2 else 0)
-            if k == 3:
-                m_t = psum.tile([P, P], F32, name="xp", bufs=2)
-                nc.tensor.transpose(m_t[:], m_wide[:], ident[:])
-                nc.scalar.copy(out=m_turn[:], in_=m_t[:])
-            if k + 1 < len(pieces):
-                stage1(k + 1, 0, 2)
-            if (first and 1 <= j and j + 2 <= LAST) or k == 2:
-                transpose_x(j + 2, 0, 2)
-                transpose_x(j + 2, 2, 4)
-            if k + 1 < len(pieces):
-                stage1(k + 1, 2, 3)
-            if k == 3:
-                nc.tensor.transpose(m_ps[:], m_turn[:], ident[:])
-            if todo:
-                empty_out(todo[0], 2 * todo[1], "s")
-                if oe == "s":
-                    empty_out(todo[0], 2 * todo[1] + 1, "s")
-            centre(k - 1, 0, width)
-            if first and j + 1 <= LAST:
-                quantize_x(j + 1)
-            if second and j + 2 <= LAST:
-                empty_x(j + 2, 0, 2, "v")
-                empty_x(j + 2, 2, 4, "v")
-            if k - 2 in (1, 2, 4, 6, 8, 10):
-                permute_c(2 + (1, 2, 4, 6, 8, 10).index(k - 2))
-            if todo:
-                if oe == "v":
-                    empty_out(todo[0], 2 * todo[1] + 1, "v")
-                store(*todo)
-            quantize_a(k - 1, 0, width)
+            hv = pieces[k][0]
+            nth = len([piece for piece in pieces[:k] if piece[0] == hv])
+            begins = nth == 0
+            middle = nth == (2 if hv == 0 else 1)
+            due = None
+            if middle and hv >= 1:
+                due = (hv - 1, 0)
+            elif begins and hv >= 2:
+                due = (hv - 2, 2)
+            elif hv == LAST and nth == 2:
+                due = (hv - 1, 2)
 
+            if due:
+                for r in (due[1], due[1] + 1):
+                    second_product(due[0], r, "cov", 2)
+            root(k, 1 if k == 2 else 0, 4)
+            if k + 1 < len(pieces):
+                first_product(k + 1, 0, 2)
+            ahead = hv + 2
+            if ahead <= LAST and (begins or k == 2):
+                turn_x(ahead, 0)
+                turn_x(ahead, 2)
+            if k + 1 < len(pieces):
+                first_product(k + 1, 2, 4)
+            if due:
+                for r in (due[1], due[1] + 1):
+                    empty_out(due[0], r)
+                store(due[0], due[1], due[1] + 2)
+
+            width = pieces[k - 1][3] - pieces[k - 1][2]
+            other = (begins and hv < LAST) or (middle and ahead <= LAST)
+            cuts = (0, width) if other else (0, width // 2, width)
+            for a, b in zip(cuts, cuts[1:]):
+                centre(k - 1, a, b)
+            if begins and hv < LAST:
+                quantize_x(hv + 1, 0, N)
+            if middle and ahead <= LAST:
+                empty_x(ahead, 0, on_vector if ahead >= 3 else on_scalar)
+                empty_x(ahead, 2, on_scalar)
+            if (begins or k == 2) and hv + 2 < GROUPS:
+                permute_c(hv + 2)
+            for a, b in zip(cuts, cuts[1:]):
+                quantize_a(k - 1, a, b)
+
+        for r in (0, 1):
+            second_product(LAST, r, "cov", 2)
+        for r in (0, 1):
+            empty_out(LAST, r)
+        store(LAST, 0, 2)
         k = len(pieces) - 1
-        stage2(LAST, 0)
-        stage2(LAST, 1)
-        empty_out(LAST, 0, "s")
-        empty_out(LAST, 1, "s")
-        store(LAST, 0)
-        centre(k, 0, 256)
-        quantize_a(k, 0, P)
-        quantize_a(k, P, 2 * P)
-        stage2(LAST, 2)
-        stage2(LAST, 3)
-        empty_out(LAST, 2, "s")
-        empty_out(LAST, 3, "v")
-        store(LAST, 1)
+        for a in (0, P):
+            centre(k, a, a + P)
+        for a in (0, P):
+            quantize_a(k, a, a + P)
+        for r in (2, 3):
+            second_product(LAST, r, "gram", 4)
+        for r in (2, 3):
+            empty_out(LAST, r)
+        for r in (2, 3):
+            store(LAST, r, r + 1)

from contextlib import ExitStack

import concourse.mybir as mybir
from concourse.masks import make_identity

F32 = mybir.dt.float32
BF16 = mybir.dt.bfloat16
I32 = mybir.dt.int32
U32 = mybir.dt.uint32
U8 = mybir.dt.uint8
FP8X4 = mybir.dt.float8_e4m3fn_x4
FP4X4 = mybir.dt.float4_e2m1fn_x4
SQRT = mybir.ActivationFunctionType.Sqrt
SUBTRACT = mybir.AluOpType.subtract

V, M, K, J, R = 4, 1024, 512, 1024, 512
P = 128
PACK = 4
N = P * PACK
HALVES = V * M // N
GROUPS = V * J // N
LAST = HALVES - 1
Q_ROWS = 4

FLOPS = 2 * V * M * J * (K + R)


def tile_landmark_distance_cross_covariance_s14_kernel(
    tc, x, c_words, c_scales, e, m, b_words, b_scales, out
):
    nc = tc.nc
    with ExitStack() as ctx:
        keep = ctx.enter_context(tc.tile_pool(name="keep", bufs=1))
        work = ctx.enter_context(tc.tile_pool(name="work", bufs=2))
        psum = ctx.enter_context(tc.psum_pool(name="psum", bufs=1))
        ctx.enter_context(tc.manual_schedule())

        ident = keep.tile([P, P], F32, name="ident")
        warm = keep.tile([P, 1], F32, name="warm")
        e_sb = keep.tile([P, GROUPS, PACK], BF16, name="e_sb")
        m_sb = keep.tile([P, GROUPS, PACK], BF16, name="m_sb")
        c_sc_raw = keep.tile([P, J], U8, name="c_sc_raw", align_bytes=64)
        c_sc = [keep.tile([P, 2, N], U8, name=f"c_sc{v}", align_bytes=64) for v in range(V)]
        b_sc = keep.tile([P, GROUPS, R], U8, name="b_sc", align_bytes=64)
        c_raw = [keep.tile([P, 2 * J], U8, name=f"c_raw{v}", align_bytes=64) for v in range(V)]
        c_codes = [keep.tile([P, 2 * N], U8, name=f"c_codes{g}", align_bytes=64) for g in range(GROUPS)]
        b_codes = [keep.tile([P, 2, 2 * R], U8, name=f"b_codes{v}", align_bytes=64) for v in range(V)]
        x_sb = [keep.tile([P, 4, K], BF16, name=f"x{hv}", align_bytes=64) for hv in range(HALVES)]

        def samples(tensor, hv):
            first = hv % 2 * N
            return tensor[hv // 2, first : first + N, :].rearrange("(p r) k -> p r k", r=4)

        def load_x(hv, r0, r1):
            nc.sync.dma_start(out=x_sb[hv][:, r0:r1, :], in_=samples(x, hv)[:, r0:r1, :])

        def load_c(v, b0, b1):
            nc.sync.dma_start(out=c_raw[v][:, b0:b1].bitcast(I32), in_=c_words[v, :, b0:b1].bitcast(I32))

        def load_c_scales():
            for q in range(4):
                nc.sync.dma_start(
                    out=c_sc_raw[32 * q : 32 * q + Q_ROWS * V].bitcast(I32),
                    in_=c_scales[:, Q_ROWS * q : Q_ROWS * (q + 1), :].bitcast(I32),
                )

        def load_b(v):
            nc.sync.dma_start(
                out=b_codes[v][:].bitcast(I32),
                in_=b_words[2 * v : 2 * v + 2].rearrange("g p n -> p g n").bitcast(I32),
            )

        def load_b_scales():
            for q in range(4):
                nc.sync.dma_start(
                    out=b_sc[32 * q : 32 * q + Q_ROWS].bitcast(I32),
                    in_=b_scales[:, Q_ROWS * q : Q_ROWS * (q + 1), :].rearrange("g r n -> r g n").bitcast(I32),
                )

        e_rows = e.rearrange("v j -> (v j)").rearrange("(g p t) -> p g t", p=P, t=PACK)
        m_rows = m.rearrange("v j -> (v j)").rearrange("(g p t) -> p g t", p=P, t=PACK)

        nc.vector.memset(c_sc_raw[:].bitcast(I32), 0)
        nc.gpsimd.memset(warm[:], 1.0)
        make_identity(nc, ident[:])
        for v in range(1, V):
            nc.gpsimd.memset(c_sc[v][:].rearrange("p h n -> p (h n)").bitcast(I32), 0)
        nc.gpsimd.memset(b_sc[:].rearrange("p g n -> p (g n)").bitcast(I32), 0)

        nc.scalar.dma_start(out=e_sb[:, :4, :], in_=e_rows[:, :4, :])
        nc.scalar.activation(out=warm[:], in_=warm[:], func=SQRT)

        load_x(0, 0, 2)
        load_c(0, 0, J)
        load_c_scales()
        load_x(0, 2, 4)
        load_c(0, J, 2 * J)
        nc.sync.dma_start(out=m_sb[:, :4, :], in_=m_rows[:, :4, :])
        load_x(1, 0, 4)
        load_c(1, 0, 2 * J)
        load_x(2, 0, 4)
        load_b(0)
        load_b_scales()
        load_x(3, 0, 4)
        nc.sync.dma_start(out=m_sb[:, 4:, :], in_=m_rows[:, 4:, :])
        nc.sync.dma_start(out=e_sb[:, 4:, :], in_=e_rows[:, 4:, :])

        def permute_c(g):
            raw = c_raw[g // 2][:, g % 2 * 2 * N : (g % 2 + 1) * 2 * N]
            nc.vector.tensor_copy(
                out=c_codes[g][:].rearrange("p (t s b) -> p t s b", t=PACK, b=2),
                in_=raw.rearrange("p (s t b) -> p t s b", t=PACK, b=2),
            )

        def permute_c_scales(h):
            nc.vector.tensor_copy(
                out=c_sc[0][:, h, :].rearrange("p (t s) -> p t s", t=PACK),
                in_=c_sc_raw[:, h * N : (h + 1) * N].rearrange("p (s t) -> p t s", t=PACK),
            )

        def spread_c_scales(v):
            for q in range(4):
                row = 32 * q + Q_ROWS * v
                nc.sync.dma_start(
                    out=c_sc[v][32 * q : 32 * q + Q_ROWS].rearrange("p h n -> p (h n)").bitcast(I32),
                    in_=c_sc[0][row : row + Q_ROWS].rearrange("p h n -> p (h n)").bitcast(I32),
                )

        turned = {}
        grouped = {}
        x_mx = {}

        def turn_x(hv, r0):
            xt = psum.tile([P, 2, 2, P], F32, name="xt", bufs=2)
            words = x_sb[hv][:].rearrange("p r k -> p (r k)").bitcast(F32)
            for r in range(2):
                start = (r0 + r) * K // 2
                for u in range(2):
                    nc.tensor.transpose(xt[:, r, u, :], words[:, start + u : start + K // 2 : 2], ident[:])
            turned[hv, r0] = xt

        def empty_x(hv, r0, copy):
            if hv not in grouped:
                grouped[hv] = work.tile([P, N, PACK], BF16, name="grouped", align_bytes=64)
            words = grouped[hv][:].rearrange("p n t -> p (n t)").bitcast(F32)
            words = words[:, r0 * 2 * P : (r0 + 2) * 2 * P].rearrange("p (r w u) -> p r w u", w=P, u=2)
            copy(out=words, in_=turned[hv, r0][:].rearrange("p r u w -> p r w u"))

        def quantize_x(hv, n0, n1):
            if hv not in x_mx:
                codes = work.tile([P, N], U32, name="x_codes", align_bytes=64)
                scales = work.tile([P, N], U8, name="x_scales", align_bytes=64)
                x_mx[hv] = (codes, scales)
            codes, scales = x_mx[hv]
            nc.vector.quantize_mx(
                out=codes[:, n0:n1].bitcast(FP8X4),
                scales=scales[:, n0:n1],
                in_=grouped[hv][:, n0:n1, :].rearrange("p n t -> p (n t)"),
            )

        pieces = [(0, 0, 0, N // 2), (0, 0, N // 2, N), (0, 1, 0, N)]
        for hv in range(1, LAST):
            pieces += [(hv, 0, 0, N), (hv, 1, 0, N)]
        pieces += [(LAST, h, n0, n0 + N // 2) for n0 in (0, N // 2) for h in (0, 1)]

        gram = {}
        dist = {}
        centred = {}
        a_mx = {}

        def group(k):
            hv, h, n0, n1 = pieces[k]
            return hv // 2 * 2 + h

        def first_product(k, t0, t1):
            hv, h, n0, n1 = pieces[k]
            codes, scales = x_mx[hv]
            for t in range(t0, t1):
                gram[k, t] = psum.tile([P, N], F32, name="gram", bufs=4)
                nc.tensor.matmul_mx(
                    out=gram[k, t][:, : n1 - n0],
                    lhsT=c_codes[group(k)][:, 2 * P * t : 2 * P * (t + 1)].bitcast(FP4X4),
                    lhsT_scale=c_sc[hv // 2][:, h, P * t : P * (t + 1)],
                    rhs=codes[:, n0:n1].bitcast(FP8X4),
                    rhs_scale=scales[:, n0:n1],
                    start=True,
                    stop=True,
                )

        def root(k, t0, t1):
            hv, h, n0, n1 = pieces[k]
            if k not in dist:
                dist[k] = work.tile([P, PACK, N], F32, name="dist", bufs=3)
            for t in range(t0, t1):
                nc.scalar.activation(
                    out=dist[k][:, t, : n1 - n0],
                    in_=gram[k, t][:, : n1 - n0],
                    func=SQRT,
                    bias=e_sb[:, group(k), t : t + 1],
                    scale=-1.0,
                )

        def centre(k, a, b):
            if k not in centred:
                centred[k] = work.tile([P, N, PACK], BF16, name="centred", align_bytes=64)
            means = m_sb[:, group(k), :].unsqueeze(1).unsqueeze(3)
            nc.vector.tensor_tensor(
                out=centred[k][:, a:b, :].rearrange("p (c i) t -> p c t i", i=2),
                in0=dist[k][:, :, a:b].rearrange("p t (c i) -> p c t i", i=2),
                in1=means.to_broadcast([P, (b - a) // 2, PACK, 2]),
                op=SUBTRACT,
            )

        def quantize_a(k, a, b):
            hv, h, n0, n1 = pieces[k]
            if (hv, h) not in a_mx:
                codes = work.tile([P, N], U32, name="a_codes", align_bytes=64, bufs=6)
                scales = work.tile([P, N], U8, name="a_scales", align_bytes=64, bufs=6)
                a_mx[hv, h] = (codes, scales)
            codes, scales = a_mx[hv, h]
            nc.vector.quantize_mx(
                out=codes[:, n0 + a : n0 + b].bitcast(FP8X4),
                scales=scales[:, n0 + a : n0 + b],
                in_=centred[k][:, a:b, :].rearrange("p n t -> p (n t)"),
            )

        cov = {}
        rows = {}

        def second_product(hv, r, name, bufs):
            cov[hv, r] = psum.tile([P, R], F32, name=name, bufs=bufs)
            for h in range(2):
                codes, scales = a_mx[hv, h]
                nc.tensor.matmul_mx(
                    out=cov[hv, r][:],
                    lhsT=codes[:, P * r : P * (r + 1)].bitcast(FP8X4),
                    lhsT_scale=scales[:, P * r : P * (r + 1)],
                    rhs=b_codes[hv // 2][:, h, :].bitcast(FP4X4),
                    rhs_scale=b_sc[:, hv // 2 * 2 + h, :],
                    start=(h == 0),
                    stop=(h == 1),
                )

        def empty_out(hv, r):
            if (hv, r // 2) not in rows:
                rows[hv, r // 2] = work.tile([P, 2, R], F32, name="rows", bufs=4)
            nc.scalar.copy(out=rows[hv, r // 2][:, r % 2, :], in_=cov[hv, r][:])

        def store(hv, r0, r1):
            part = rows[hv, r0 // 2][:, r0 % 2 : r0 % 2 + r1 - r0, :]
            nc.sync.dma_start(out=samples(out, hv)[:, r0:r1, :], in_=part)

        on_vector = nc.vector.tensor_copy
        on_scalar = nc.scalar.copy

        turn_x(0, 0)
        turn_x(0, 2)
        permute_c(0)
        permute_c_scales(0)
        empty_x(0, 0, on_scalar)
        quantize_x(0, 0, N // 2)
        first_product(0, 0, 4)
        root(0, 0, 4)
        empty_x(0, 2, on_vector)
        permute_c_scales(1)
        quantize_x(0, N // 2, N)
        permute_c(1)
        first_product(1, 0, 4)
        for v in range(1, V):
            spread_c_scales(v)
        load_c(2, 0, 2 * J)
        load_c(3, 0, 2 * J)
        for hv in range(4, HALVES):
            load_x(hv, 0, 4)
            if hv % 2 == 0:
                load_b(hv // 2 - 1)
        load_b(3)
        root(1, 0, 4)
        first_product(2, 0, 1)
        turn_x(1, 0)
        turn_x(1, 2)
        first_product(2, 1, 4)
        centre(0, 0, N // 2)
        root(2, 0, 1)
        empty_x(1, 0, on_vector)
        empty_x(1, 2, on_scalar)
        quantize_a(0, 0, N // 2)
        quantize_x(1, 0, N)

        for k in range(2, len(pieces)):
            hv = pieces[k][0]
            nth = len([piece for piece in pieces[:k] if piece[0] == hv])
            begins = nth == 0
            middle = nth == (2 if hv == 0 else 1)
            due = None
            if middle and hv >= 1:
                due = (hv - 1, 0)
            elif begins and hv >= 2:
                due = (hv - 2, 2)
            elif hv == LAST and nth == 2:
                due = (hv - 1, 2)

            if due:
                for r in (due[1], due[1] + 1):
                    second_product(due[0], r, "cov", 2)
            root(k, 1 if k == 2 else 0, 4)
            if k + 1 < len(pieces):
                first_product(k + 1, 0, 2)
            ahead = hv + 2
            if ahead <= LAST and (begins or k == 2):
                turn_x(ahead, 0)
                turn_x(ahead, 2)
            if k + 1 < len(pieces):
                first_product(k + 1, 2, 4)
            if due:
                for r in (due[1], due[1] + 1):
                    empty_out(due[0], r)
                store(due[0], due[1], due[1] + 2)

            width = pieces[k - 1][3] - pieces[k - 1][2]
            other = (begins and hv < LAST) or (middle and ahead <= LAST)
            cuts = (0, width) if other else (0, width // 2, width)
            for a, b in zip(cuts, cuts[1:]):
                centre(k - 1, a, b)
            if begins and hv < LAST:
                quantize_x(hv + 1, 0, N)
            if middle and ahead <= LAST:
                empty_x(ahead, 0, on_vector if ahead >= 3 else on_scalar)
                empty_x(ahead, 2, on_scalar)
            if (begins or k == 2) and hv + 2 < GROUPS:
                permute_c(hv + 2)
            for a, b in zip(cuts, cuts[1:]):
                quantize_a(k - 1, a, b)

        for r in (0, 1):
            second_product(LAST, r, "cov", 2)
        for r in (0, 1):
            empty_out(LAST, r)
        store(LAST, 0, 2)
        k = len(pieces) - 1
        for a in (0, P):
            centre(k, a, a + P)
        for a in (0, P):
            quantize_a(k, a, a + P)
        for r in (2, 3):
            second_product(LAST, r, "gram", 4)
        for r in (2, 3):
            empty_out(LAST, r)
        for r in (2, 3):
            store(LAST, r, r + 1)
